import numpy as np
CORES = [7,6,5,4,3,2,1,0]
N = 8
ROOT = 7
def setup_inputs(rng):
    return {"x": rng.standard_normal((N, 128, N * 1024), dtype=np.float32)}
def reference(x):
    return {"y": np.stack([x[ROOT][:, r * 1024:(r + 1) * 1024] for r in range(N)])}

from concourse.bass import DstId, RemoteDMATransfer

BLOCK = 1024
PEERS = 7
ENGINES = 2

SCRATCH = {
    "stage": ("sbuf", [128, PEERS * BLOCK], "float32"),
    "land": ("sbuf", [128, BLOCK], "float32"),
}
SEMAPHORES = ["loaded", "stored", "sent", "arrived"]


def rank_program(g, core, T, topo):
    rank = T.rank_of(core)
    if rank is None:
        return
    root = T.root

    if rank != root:
        g.wait_ge(T.sem.arrived, ENGINES)
        g.dma_start(T.y[:, :], T.land[:, :]).then_inc(T.sem.stored, 16)
        g.wait_ge(T.sem.stored, 16)
        return

    peers = [r for r in range(len(T.cores)) if r != root]

    g.dma_start(T.y[:, :], T.x[:, root * BLOCK:(root + 1) * BLOCK]).then_inc(T.sem.stored, 16)

    loads = 0
    below = root * BLOCK
    total = len(peers) * BLOCK
    if below > 0:
        g.dma_start(T.stage[:, 0:below], T.x[:, 0:below]).then_inc(T.sem.loaded, 16)
        loads += 1
    if below < total:
        g.dma_start(T.stage[:, below:total], T.x[:, below + BLOCK:total + BLOCK]).then_inc(T.sem.loaded, 16)
        loads += 1
    g.wait_ge(T.sem.loaded, 16 * loads)

    transfers = []
    for k, r in enumerate(peers):
        dst = T.cores[r]
        where = topo.addr(dst)
        pair = ((1 << ENGINES) - 1) << (ENGINES * k)
        transfers.append(RemoteDMATransfer(
            dst_ids=[DstId(rid=where[0], pnc=where[1])],
            dma_engine_mask=pair & topo.mask(core, dst),
            remote_sem=T.sem.arrived,
            src=T.stage[:, k * BLOCK:(k + 1) * BLOCK],
            dst=T.land[:, :],
        ))
    g.remote_dma_fused(transfers, local_sem=T.sem.sent)

    g.wait_ge(T.sem.sent, ENGINES * len(peers))
    g.wait_ge(T.sem.stored, 16)
